import numpy as np
import ml_dtypes


def mxq(x, axis, fmt="e4m3"):
    dtype, down = {"e4m3": (ml_dtypes.float8_e4m3fn, 7), "e5m2": (ml_dtypes.float8_e5m2, 14)}[fmt]
    v = np.moveaxis(np.asarray(x, np.float32).astype(ml_dtypes.bfloat16).astype(np.float64), axis, -1)
    blocks = v.reshape(v.shape[:-1] + (-1, 32))
    amax = np.abs(blocks).max(-1, keepdims=True)
    byte = np.maximum(np.where(amax > 0, np.frexp(amax)[1] - 1 + 127, 0) - down, 1)
    scale = np.exp2(byte - 127.0)
    codes = (blocks / scale).astype(np.float32).astype(dtype).astype(np.float64)
    return np.moveaxis((codes * scale).reshape(v.shape), -1, axis)


WIDE = False


def mx_kscale(k):
    if not WIDE:
        return np.ones(k)
    levels = np.array([10, -10, 5, -5, 0])
    if k % 512:
        return np.exp2(np.random.permutation(np.resize(levels, k // 32))).repeat(32)
    a = np.empty((k // 512, 16))
    for p in range(k // 512):
        a[p, :8] = np.random.permutation(np.resize(levels, 8))
        for g in range(8):
            far = levels[np.abs(levels - a[p, g]) >= 10]
            a[p, g + 8] = far[np.random.randint(len(far))]
    return np.exp2(a.ravel()).repeat(32)


def f64(x):
    return np.asarray(x).astype(np.float64)


def striped(idx):
    return np.tile(idx.reshape(-1, 16).T, (8, 1)).astype(np.uint16)


def unstriped(offs):
    return offs[:16].T.reshape(-1).astype(np.int64)


E2M1 = np.array([0.0, 0.5, 1.0, 1.5, 2.0, 3.0, 4.0, 6.0, -0.0, -0.5, -1.0, -1.5, -2.0, -3.0, -4.0, -6.0])


def pack_weight(w, fmt):
    k, n = w.shape
    w = f64(np.asarray(w, np.float32).astype(ml_dtypes.bfloat16)).reshape(k // 32, 32, n)
    amax = np.abs(w).max(1)
    if fmt == "e4m3":
        byte = np.frexp(amax)[1] - 1 + 127 - 7
    else:
        mant, ex = np.frexp(amax / 6.0)
        byte = np.where(mant > 0.5, ex, ex - 1) + 127
    byte = np.clip(np.where(amax > 0, byte, 1), 1, 254)
    scaled = (w * np.exp2(127.0 - byte)[:, None, :]).reshape(k, n).astype(np.float32)
    by_word = np.ascontiguousarray(scaled.reshape(k // 512, 128, 4, n).transpose(0, 1, 3, 2))
    if fmt == "e4m3":
        words = by_word.astype(ml_dtypes.float8_e4m3fn).view(np.uint8)
    else:
        c = by_word.astype(ml_dtypes.float4_e2m1fn).view(np.uint8) & 0xF
        words = (c[..., 0::2] | (c[..., 1::2] << 4)).reshape(k // 512, 128, 2 * n)
    return np.ascontiguousarray(words), np.ascontiguousarray(byte.astype(np.uint8).reshape(k // 512, 16, n))


def unpack_weight(words, scales, fmt):
    g, _, n = scales.shape
    words = np.ascontiguousarray(words).reshape(g, 128, n, -1)
    if fmt == "e4m3":
        vals = words.view(ml_dtypes.float8_e4m3fn).astype(np.float64)
    else:
        nib = np.empty((g, 128, n, 4), np.uint8)
        nib[..., 0::2] = words & 0xF
        nib[..., 1::2] = words >> 4
        vals = E2M1[nib]
    vals = vals * np.repeat(np.exp2(scales.astype(np.float64) - 127.0), 8, axis=1)[..., None]
    return vals.transpose(0, 1, 3, 2).reshape(g * 512, n)


def gelu(v):
    return 0.5 * v * (1.0 + np.tanh(np.sqrt(2.0 / np.pi) * (v + 0.044715 * v**3)))


def twice(P):
    return np.random.permutation(np.repeat(np.arange(P), 2))


K, H, T, S, P = 512, 1024, 4096, 1024, 512


def setup_inputs():
    n = np.random.standard_normal
    s = mx_kscale(K)[:, None]
    u = mx_kscale(H)[:, None]
    d = {}
    d["tab_words"], d["tab_scales"] = pack_weight(n((K, T)) * s, "e4m3")
    d["offs"] = striped(np.random.permutation(T)[:S])
    d["w4_words"], d["w4_scales"] = pack_weight(n((K, H)) / K ** 0.5 / s * u.T, "e2m1")
    d["w2"] = (0.9 * n((K, H)) / K ** 0.5 / s * np.sqrt(u).T).astype(np.float32)
    d["pos1"] = striped(np.random.permutation(S)[:P])
    d["pos2"] = striped(np.random.permutation(S)[:P])
    d["w3"] = (0.45 * n((H, H)) / H ** 0.5 / u).astype(np.float32)
    d["pos3"] = striped(twice(P))
    d["gain"] = (0.6 * np.exp(0.3 * n(H)) / u[:, 0]).astype(np.float32)
    return d


def reference(tab_words, tab_scales, offs, w4_words, w4_scales, w2, pos1, pos2, w3, pos3, gain):
    v = unpack_weight(tab_words, tab_scales, "e4m3")[:, unstriped(offs)]
    w4 = unpack_weight(w4_words, w4_scales, "e2m1")
    a = w4.T @ v
    b = mxq(f64(w2), 0, "e4m3").T @ v
    h = a + np.square(b)
    z = h[:, unstriped(pos1)] - h[:, unstriped(pos2)]
    y = mxq(f64(w3), 0, "e4m3").T @ mxq(z, 0, "e4m3")
    up = y[:, unstriped(pos3)]
    return np.abs(up) * (h * f64(gain)[:, None]) + up

@@ -1,0 +1,253 @@
+from contextlib import ExitStack
+
+import concourse.mybir as mybir
+
+K, H, T, S, M = 512, 1024, 4096, 1024, 512
+FLOPS = 2 * (2 * K * H * S + H * H * M)
+
+F32 = mybir.dt.float32
+BF16 = mybir.dt.bfloat16
+I32 = mybir.dt.int32
+U32 = mybir.dt.uint32
+U16 = mybir.dt.uint16
+U8 = mybir.dt.uint8
+E4M3 = mybir.dt.float8_e4m3fn_x4
+E2M1 = mybir.dt.float4_e2m1fn_x4
+ALU = mybir.AluOpType
+ACT = mybir.ActivationFunctionType
+
+P = 128
+PACK = 4
+PASS = P * PACK
+BANK = 512
+TILES = H // P
+Y_WINDOW = 1536
+
+
+def tile_list_loft_return_scores_kernel(
+    tc, tab_words, tab_scales, offs, w4_words, w4_scales, w2, pos1, pos2, w3, pos3, gain, out
+):
+    nc = tc.nc
+    with ExitStack() as ctx:
+        keep = ctx.enter_context(tc.tile_pool(name="keep", bufs=1))
+        ring = ctx.enter_context(tc.tile_pool(name="ring", bufs=2))
+        psum = ctx.enter_context(tc.psum_pool(name="psum", bufs=1))
+
+        offs_t = keep.tile([P, S // 16], U16, name="offs_t")
+        pos1_t = keep.tile([P, M // 16], U16, name="pos1_t")
+        pos2_t = keep.tile([P, M // 16], U16, name="pos2_t")
+        pos3_t = keep.tile([P, S // 16], U16, name="pos3_t")
+        tabw = keep.tile([P, T], I32, name="tabw", align_bytes=64)
+        tabs = keep.tile([P, T], U8, name="tabs", align_bytes=64)
+        w4w_raw = keep.tile([P, 2 * H], U8, name="w4w_raw", align_bytes=64)
+        w4s_raw = keep.tile([P, H], U8, name="w4s_raw", align_bytes=64)
+        gain_t = keep.tile([P, 2, PACK], F32, name="gain_t")
+        ys = keep.tile([P, (TILES - 1) * M + Y_WINDOW], F32, name="ys")
+
+        nc.gpsimd.memset(w4s_raw[:].bitcast(I32), 0)
+        nc.vector.memset(tabs[:].bitcast(I32), 0)
+        nc.sync.dma_start(offs_t[:], offs)
+        nc.sync.dma_start(out=w4w_raw[:].bitcast(I32), in_=w4_words[0].bitcast(I32))
+        for plane, rows in ((tabs, tab_scales), (w4s_raw, w4_scales)):
+            for q in range(4):
+                nc.sync.dma_start(
+                    out=plane[32 * q : 32 * q + 4, :].bitcast(I32),
+                    in_=rows[0, 4 * q : 4 * q + 4, :].bitcast(I32),
+                )
+        nc.sync.dma_start(out=tabw[:], in_=tab_words[0].rearrange("p t i -> p (t i)").bitcast(I32))
+        nc.gpsimd.memset(ys[:, TILES * M :], 0.0)
+
+        def load_weight(rows, b, name):
+            raw = ring.tile([P, PACK, PASS], F32, name=name, tag="raw", bufs=4)
+            nc.sync.dma_start(
+                out=raw[:], in_=rows.rearrange("(p j) n -> p j n", j=PACK)[:, :, b * PASS : (b + 1) * PASS]
+            )
+            return raw
+
+        def round_weight(raw, name, split):
+            grouped = ring.tile([P, PACK * PASS], BF16, name=name, tag="grouped", bufs=2, align_bytes=64)
+            dst = grouped[:].rearrange("p (t q j) -> p q j t", t=PACK, j=PACK)
+            src = raw[:].rearrange("p j (q t) -> p q j t", t=PACK)
+            for engine, q0, q1 in split:
+                if engine == "v":
+                    nc.vector.tensor_copy(out=dst[:, q0:q1], in_=src[:, q0:q1])
+                else:
+                    nc.scalar.copy(out=dst[:, q0:q1], in_=src[:, q0:q1])
+            return grouped
+
+        def mx_tiles(name, cols):
+            codes = keep.tile([P, cols], U32, name=name + "_codes", align_bytes=64)
+            scales = keep.tile([P, cols], U8, name=name + "_scales", align_bytes=64)
+            return codes, scales
+
+        def quantize(mx, grouped, c0, c1):
+            codes, scales = mx
+            nc.vector.quantize_mx(
+                out=codes[:, c0:c1].bitcast(E4M3), scales=scales[:, c0:c1], in_=grouped[:, PACK * c0 : PACK * c1]
+            )
+
+        w2_raw = [load_weight(w2, b, "w2_raw%d" % b) for b in range(2)]
+        nc.sync.dma_start(pos2_t[:], pos2)
+        nc.sync.dma_start(pos1_t[:], pos1)
+        w3_raw = {}
+        for b in range(2):
+            for a in range(2):
+                w3_raw[a, b] = load_weight(w3[a * PASS : (a + 1) * PASS, :], b, "w3_raw%d%d" % (a, b))
+            if b == 0:
+                nc.sync.dma_start(pos3_t[:], pos3)
+                nc.sync.dma_start(out=gain_t[:], in_=gain.rearrange("(b p t) -> p b t", b=2, t=PACK))
+
+        vw = [keep.tile([P, BANK], U32, name="vw%d" % u, align_bytes=64) for u in range(2)]
+        vs = keep.tile([P, S], U8, name="vs", align_bytes=64)
+        nc.vector.tensor_copy(vs[:], tabs[:].indirect(offs_t[:]))
+
+        w4w = [keep.tile([P, 2 * PASS], U8, name="w4w%d" % b, align_bytes=64) for b in range(2)]
+        w4s = [keep.tile([P, PASS], U8, name="w4s%d" % b, align_bytes=64) for b in range(2)]
+        for b in range(2):
+            nc.vector.tensor_copy(
+                out=w4w[b][:].rearrange("p (t q e) -> p t q e", t=PACK, e=2),
+                in_=w4w_raw[:, 2 * PASS * b : 2 * PASS * (b + 1)].rearrange("p (q t e) -> p t q e", t=PACK, e=2),
+            )
+            nc.vector.tensor_copy(
+                out=w4s[b][:].rearrange("p (t q) -> p t q", t=PACK),
+                in_=w4s_raw[:, PASS * b : PASS * (b + 1)].rearrange("p (q t) -> p t q", t=PACK),
+            )
+        for u in range(2):
+            nc.vector.tensor_copy(vw[u][:], tabw[:].bitcast(U32).indirect(offs_t[:, 32 * u : 32 * (u + 1)]))
+
+        w2q = [mx_tiles("w2q%d" % b, PASS) for b in range(2)]
+        w3q = {(a, b): mx_tiles("w3q%d%d" % (a, b), PASS) for a in range(2) for b in range(2)}
+        zq = [mx_tiles("zq%d" % a, M) for a in range(2)]
+
+        grouped = round_weight(w2_raw[0], "w2_g0", [("v", 0, 80), ("s", 80, 128)])
+        quantize(w2q[0], grouped, 0, P)
+        quantize(w2q[0], grouped, P, 2 * P)
+        quantize(w2q[0], grouped, 2 * P, 4 * P)
+
+        h = [keep.tile([P, S], F32, name="h%d" % i) for i in range(TILES)]
+        z32 = [keep.tile([P, PACK, M], F32, name="z32_%d" % a) for a in range(2)]
+        zg = [keep.tile([P, PACK * M], BF16, name="zg%d" % a, align_bytes=64) for a in range(2)]
+
+        def make_h(i, u):
+            b, t = divmod(i, PACK)
+            cols = slice(u * BANK, (u + 1) * BANK)
+            pa = psum.tile([P, BANK], F32, name="pa", tag="pa", bufs=3)
+            pb = psum.tile([P, BANK], F32, name="pb", tag="pb", bufs=3)
+            codes, scales = w2q[b]
+            nc.tensor.matmul_mx(
+                out=pb[:], lhsT=codes[:, t * P : (t + 1) * P].bitcast(E4M3), lhsT_scale=scales[:, t * P : (t + 1) * P],
+                rhs=vw[u][:].bitcast(E4M3), rhs_scale=vs[:, cols], start=True, stop=True,
+            )
+            nc.tensor.matmul_mx(
+                out=pa[:], lhsT=w4w[b][:, 2 * t * P : 2 * (t + 1) * P].bitcast(E2M1),
+                lhsT_scale=w4s[b][:, t * P : (t + 1) * P],
+                rhs=vw[u][:].bitcast(E4M3), rhs_scale=vs[:, cols], start=True, stop=True,
+            )
+            sq = ring.tile([P, BANK], F32, name="sq", tag="sq", bufs=3)
+            nc.scalar.activation(sq[:], pb[:], ACT.Square)
+            nc.vector.tensor_tensor(h[i][:, cols], pa[:], sq[:], ALU.add)
+
+        def pick_second(i, m0, m1):
+            second = ring.tile([P, M], F32, name="second", tag="second", bufs=2)
+            nc.vector.tensor_copy(second[:, 0 : m1 - m0], h[i][:].indirect(pos2_t[:, m0 // 16 : m1 // 16]))
+            return second
+
+        def pick_difference(i, second, m0, m1):
+            b, t = divmod(i, PACK)
+            nc.vector.tensor_tensor(
+                z32[b][:, t, m0:m1], h[i][:].indirect(pos1_t[:, m0 // 16 : m1 // 16]), second[:, 0 : m1 - m0],
+                ALU.subtract,
+            )
+
+        def round_z(a, m0, m1):
+            nc.scalar.copy(
+                out=zg[a][:, PACK * m0 : PACK * m1].rearrange("p (c i t) -> p c t i", i=4, t=PACK),
+                in_=z32[a][:, :, m0:m1].rearrange("p t (c i) -> p c t i", i=4),
+            )
+
+        halves = [("s", 0, 64), ("s", 64, 128)]
+        make_h(0, 0)
+        make_h(0, 1)
+        w3_grouped = {}
+        for i in range(TILES - 1):
+            make_h(i + 1, 0)
+            second = pick_second(i, 0, M)
+            make_h(i + 1, 1)
+            pick_difference(i, second, 0, M)
+            if i == 0:
+                grouped = round_weight(w2_raw[1], "w2_g1", halves)
+            if i == 1:
+                quantize(w2q[1], grouped, 0, PASS)
+            if i == 3:
+                round_z(0, 0, M // 2)
+                round_z(0, M // 2, M)
+            if i == 4:
+                quantize(zq[0], zg[0], 0, M)
+            if i in (1, 2):
+                w3_grouped[i - 1, 0] = round_weight(w3_raw[i - 1, 0], "w3_g%d0" % (i - 1), halves)
+            if i in (2, 3):
+                quantize(w3q[i - 2, 0], w3_grouped[i - 2, 0], 0, PASS)
+            if i in (4, 5):
+                w3_grouped[i - 4, 1] = round_weight(w3_raw[i - 4, 1], "w3_g%d1" % (i - 4), halves)
+        last = TILES - 1
+        seconds = [pick_second(last, u * M // 2, (u + 1) * M // 2) for u in range(2)]
+        for u in range(2):
+            pick_difference(last, seconds[u], u * M // 2, (u + 1) * M // 2)
+            round_z(1, u * M // 2, (u + 1) * M // 2)
+        quantize(w3q[0, 1], w3_grouped[0, 1], 0, PASS)
+        quantize(zq[1], zg[1], 0, M // 2)
+        quantize(w3q[1, 1], w3_grouped[1, 1], 0, PASS)
+        quantize(zq[1], zg[1], M // 2, M)
+
+        out_tiles = out.rearrange("(b p t) j -> b t p j", b=2, t=PACK)
+
+        def make_y(n):
+            b, t = divmod(n, PACK)
+            py = psum.tile([P, M], F32, name="py", tag="py", bufs=2)
+            for a in range(2):
+                codes, scales = w3q[a, b]
+                nc.tensor.matmul_mx(
+                    out=py[:], lhsT=codes[:, t * P : (t + 1) * P].bitcast(E4M3),
+                    lhsT_scale=scales[:, t * P : (t + 1) * P],
+                    rhs=zq[a][0][:].bitcast(E4M3), rhs_scale=zq[a][1][:], start=(a == 0), stop=(a == 1),
+                )
+            y0 = (TILES - 1 - n) * M
+            nc.scalar.copy(out=ys[:, y0 : y0 + M], in_=py[:])
+
+        pieces = [(n, 0, S) for n in range(TILES - 1)] + [(last, 0, S // 2), (last, S // 2, S)]
+        ups = {}
+        mags = {}
+
+        def pick_up(k):
+            n, j0, j1 = pieces[k]
+            y0 = (TILES - 1 - n) * M
+            up = ring.tile([P, S], F32, name="up", tag="up", bufs=4)
+            nc.vector.tensor_copy(up[:, 0 : j1 - j0], ys[:, y0 : y0 + Y_WINDOW].indirect(pos3_t[:, j0 // 16 : j1 // 16]))
+            mag = ring.tile([P, S], F32, name="mag", tag="mag", bufs=3)
+            nc.scalar.activation(mag[:, 0 : j1 - j0], up[:, 0 : j1 - j0], ACT.Abs)
+            ups[k], mags[k] = up, mag
+
+        def scale_up(k):
+            n, j0, j1 = pieces[k]
+            b, t = divmod(n, PACK)
+            mag = mags[k][:, 0 : j1 - j0]
+            nc.vector.scalar_tensor_tensor(mag, mag, gain_t[:, b, t : t + 1], h[n][:, j0:j1], ALU.mult, ALU.mult)
+
+        def finish(k):
+            n, j0, j1 = pieces[k]
+            b, t = divmod(n, PACK)
+            up = ups[k][:, 0 : j1 - j0]
+            nc.vector.tensor_tensor(up, mags[k][:, 0 : j1 - j0], up, ALU.add)
+            nc.sync.dma_start(out=out_tiles[b, t][:, j0:j1], in_=up)
+
+        make_y(0)
+        make_y(1)
+        for k in range(len(pieces) + 2):
+            if k + 2 < TILES:
+                make_y(k + 2)
+            if k < len(pieces):
+                pick_up(k)
+            if 2 <= k:
+                finish(k - 2)
+            if 1 <= k <= len(pieces):
+                scale_up(k - 1)

@@ -1,6 +1,7 @@
 from contextlib import ExitStack
 
 import concourse.mybir as mybir
+from concourse.masks import make_identity
 
 K, H, T, S, M = 512, 1024, 4096, 1024, 512
 FLOPS = 2 * (2 * K * H * S + H * H * M)
@@ -44,18 +45,23 @@ def tile_list_loft_return_scores_kernel(
         gain_t = keep.tile([P, 2, PACK], F32, name="gain_t")
         ys = keep.tile([P, (TILES - 1) * M + Y_WINDOW], F32, name="ys")
 
+        nc.gpsimd.memset(tabs[:].bitcast(I32)[:, 0:640], 0)
+        nc.vector.memset(tabs[:].bitcast(I32)[:, 640:], 0)
         nc.gpsimd.memset(w4s_raw[:].bitcast(I32), 0)
-        nc.vector.memset(tabs[:].bitcast(I32), 0)
         nc.sync.dma_start(offs_t[:], offs)
         nc.sync.dma_start(out=w4w_raw[:].bitcast(I32), in_=w4_words[0].bitcast(I32))
-        for plane, rows in ((tabs, tab_scales), (w4s_raw, w4_scales)):
+
+        def load_scale_rows(engine, plane, rows):
             for q in range(4):
-                nc.sync.dma_start(
-                    out=plane[32 * q : 32 * q + 4, :].bitcast(I32),
-                    in_=rows[0, 4 * q : 4 * q + 4, :].bitcast(I32),
+                engine.dma_start(
+                    out=plane[32 * q : 32 * q + 4, :].bitcast(I32), in_=rows[0, 4 * q : 4 * q + 4, :].bitcast(I32)
                 )
+
+        load_scale_rows(nc.sync, tabs, tab_scales)
         nc.sync.dma_start(out=tabw[:], in_=tab_words[0].rearrange("p t i -> p (t i)").bitcast(I32))
         nc.gpsimd.memset(ys[:, TILES * M :], 0.0)
+        ident = keep.tile([P, P], F32, name="ident")
+        make_identity(nc, ident[:])
 
         def load_weight(rows, b, name):
             raw = ring.tile([P, PACK, PASS], F32, name=name, tag="raw", bufs=4)
@@ -65,7 +71,7 @@ def tile_list_loft_return_scores_kernel(
             return raw
 
         def round_weight(raw, name, split):
-            grouped = ring.tile([P, PACK * PASS], BF16, name=name, tag="grouped", bufs=2, align_bytes=64)
+            grouped = ring.tile([P, PACK * PASS], BF16, name=name, tag="grouped", bufs=4, align_bytes=64)
             dst = grouped[:].rearrange("p (t q j) -> p q j t", t=PACK, j=PACK)
             src = raw[:].rearrange("p j (q t) -> p q j t", t=PACK)
             for engine, q0, q1 in split:
@@ -86,7 +92,9 @@ def tile_list_loft_return_scores_kernel(
                 out=codes[:, c0:c1].bitcast(E4M3), scales=scales[:, c0:c1], in_=grouped[:, PACK * c0 : PACK * c1]
             )
 
-        w2_raw = [load_weight(w2, b, "w2_raw%d" % b) for b in range(2)]
+        w2_raw = [load_weight(w2, 0, "w2_raw0")]
+        load_scale_rows(nc.sync, w4s_raw, w4_scales)
+        w2_raw.append(load_weight(w2, 1, "w2_raw1"))
         nc.sync.dma_start(pos2_t[:], pos2)
         nc.sync.dma_start(pos1_t[:], pos1)
         w3_raw = {}
@@ -97,21 +105,23 @@ def tile_list_loft_return_scores_kernel(
                 nc.sync.dma_start(pos3_t[:], pos3)
                 nc.sync.dma_start(out=gain_t[:], in_=gain.rearrange("(b p t) -> p b t", b=2, t=PACK))
 
-        vw = [keep.tile([P, BANK], U32, name="vw%d" % u, align_bytes=64) for u in range(2)]
-        vs = keep.tile([P, S], U8, name="vs", align_bytes=64)
-        nc.vector.tensor_copy(vs[:], tabs[:].indirect(offs_t[:]))
-
         w4w = [keep.tile([P, 2 * PASS], U8, name="w4w%d" % b, align_bytes=64) for b in range(2)]
         w4s = [keep.tile([P, PASS], U8, name="w4s%d" % b, align_bytes=64) for b in range(2)]
         for b in range(2):
             nc.vector.tensor_copy(
-                out=w4w[b][:].rearrange("p (t q e) -> p t q e", t=PACK, e=2),
-                in_=w4w_raw[:, 2 * PASS * b : 2 * PASS * (b + 1)].rearrange("p (q t e) -> p t q e", t=PACK, e=2),
+                out=w4w[b][:].bitcast(U16).rearrange("p (t q) -> p t q", t=PACK),
+                in_=w4w_raw[:, 2 * PASS * b : 2 * PASS * (b + 1)].bitcast(U16).rearrange("p (q t) -> p t q", t=PACK),
             )
+
+        def deal_w4_scales(b):
             nc.vector.tensor_copy(
                 out=w4s[b][:].rearrange("p (t q) -> p t q", t=PACK),
                 in_=w4s_raw[:, PASS * b : PASS * (b + 1)].rearrange("p (q t) -> p t q", t=PACK),
             )
+
+        vw = [keep.tile([P, BANK], U32, name="vw%d" % u, align_bytes=64) for u in range(2)]
+        vs = keep.tile([P, S], U8, name="vs", align_bytes=64)
+        nc.vector.tensor_copy(vs[:], tabs[:].indirect(offs_t[:]))
         for u in range(2):
             nc.vector.tensor_copy(vw[u][:], tabw[:].bitcast(U32).indirect(offs_t[:, 32 * u : 32 * (u + 1)]))
 
@@ -121,6 +131,7 @@ def tile_list_loft_return_scores_kernel(
 
         grouped = round_weight(w2_raw[0], "w2_g0", [("v", 0, 80), ("s", 80, 128)])
         quantize(w2q[0], grouped, 0, P)
+        deal_w4_scales(0)
         quantize(w2q[0], grouped, P, 2 * P)
         quantize(w2q[0], grouped, 2 * P, 4 * P)
 
@@ -128,27 +139,30 @@ def tile_list_loft_return_scores_kernel(
         z32 = [keep.tile([P, PACK, M], F32, name="z32_%d" % a) for a in range(2)]
         zg = [keep.tile([P, PACK * M], BF16, name="zg%d" % a, align_bytes=64) for a in range(2)]
 
-        def make_h(i, u):
+        def square_part(i, u):
             b, t = divmod(i, PACK)
             cols = slice(u * BANK, (u + 1) * BANK)
-            pa = psum.tile([P, BANK], F32, name="pa", tag="pa", bufs=3)
             pb = psum.tile([P, BANK], F32, name="pb", tag="pb", bufs=3)
             codes, scales = w2q[b]
             nc.tensor.matmul_mx(
                 out=pb[:], lhsT=codes[:, t * P : (t + 1) * P].bitcast(E4M3), lhsT_scale=scales[:, t * P : (t + 1) * P],
                 rhs=vw[u][:].bitcast(E4M3), rhs_scale=vs[:, cols], start=True, stop=True,
             )
+            nc.scalar.activation(h[i][:, cols], pb[:], ACT.Square)
+
+        def linear_part(i, u):
+            b, t = divmod(i, PACK)
+            cols = slice(u * BANK, (u + 1) * BANK)
+            pa = psum.tile([P, BANK], F32, name="pa", tag="pa", bufs=3)
             nc.tensor.matmul_mx(
                 out=pa[:], lhsT=w4w[b][:, 2 * t * P : 2 * (t + 1) * P].bitcast(E2M1),
                 lhsT_scale=w4s[b][:, t * P : (t + 1) * P],
                 rhs=vw[u][:].bitcast(E4M3), rhs_scale=vs[:, cols], start=True, stop=True,
             )
-            sq = ring.tile([P, BANK], F32, name="sq", tag="sq", bufs=3)
-            nc.scalar.activation(sq[:], pb[:], ACT.Square)
-            nc.vector.tensor_tensor(h[i][:, cols], pa[:], sq[:], ALU.add)
+            nc.vector.tensor_tensor(h[i][:, cols], pa[:], h[i][:, cols], ALU.add)
 
         def pick_second(i, m0, m1):
-            second = ring.tile([P, M], F32, name="second", tag="second", bufs=2)
+            second = ring.tile([P, M], F32, name="second", tag="second", bufs=3)
             nc.vector.tensor_copy(second[:, 0 : m1 - m0], h[i][:].indirect(pos2_t[:, m0 // 16 : m1 // 16]))
             return second
 
@@ -159,95 +173,136 @@ def tile_list_loft_return_scores_kernel(
                 ALU.subtract,
             )
 
-        def round_z(a, m0, m1):
-            nc.scalar.copy(
+        def round_z(a, m0, m1, copy):
+            copy(
                 out=zg[a][:, PACK * m0 : PACK * m1].rearrange("p (c i t) -> p c t i", i=4, t=PACK),
                 in_=z32[a][:, :, m0:m1].rearrange("p t (c i) -> p c t i", i=4),
             )
 
-        halves = [("s", 0, 64), ("s", 64, 128)]
-        make_h(0, 0)
-        make_h(0, 1)
+        whole = [("s", 0, P)]
+        for u in range(2):
+            square_part(0, u)
+            linear_part(0, u)
+        for u in range(2):
+            square_part(1, u)
+        w2_grouped = round_weight(w2_raw[1], "w2_g1", whole)
+        for i in (2, 3):
+            for u in range(2):
+                square_part(i, u)
         w3_grouped = {}
         for i in range(TILES - 1):
-            make_h(i + 1, 0)
+            linear_part(i + 1, 0)
             second = pick_second(i, 0, M)
-            make_h(i + 1, 1)
+            linear_part(i + 1, 1)
             pick_difference(i, second, 0, M)
             if i == 0:
-                grouped = round_weight(w2_raw[1], "w2_g1", halves)
-            if i == 1:
-                quantize(w2q[1], grouped, 0, PASS)
+                quantize(w2q[1], w2_grouped, 0, PASS)
+                deal_w4_scales(1)
+                for r in range(PACK, TILES):
+                    for u in range(2):
+                        square_part(r, u)
+                for a in range(2):
+                    w3_grouped[a, 0] = round_weight(w3_raw[a, 0], "w3_g%d0" % a, whole)
             if i == 3:
-                round_z(0, 0, M // 2)
-                round_z(0, M // 2, M)
-            if i == 4:
+                round_z(0, 0, M, nc.scalar.copy)
+                for a in range(2):
+                    w3_grouped[a, 1] = round_weight(w3_raw[a, 1], "w3_g%d1" % a, whole)
+            if i in (3, 4):
+                quantize(w3q[i - 3, 0], w3_grouped[i - 3, 0], 0, PASS)
+            if i == 5:
                 quantize(zq[0], zg[0], 0, M)
-            if i in (1, 2):
-                w3_grouped[i - 1, 0] = round_weight(w3_raw[i - 1, 0], "w3_g%d0" % (i - 1), halves)
-            if i in (2, 3):
-                quantize(w3q[i - 2, 0], w3_grouped[i - 2, 0], 0, PASS)
-            if i in (4, 5):
-                w3_grouped[i - 4, 1] = round_weight(w3_raw[i - 4, 1], "w3_g%d1" % (i - 4), halves)
         last = TILES - 1
-        seconds = [pick_second(last, u * M // 2, (u + 1) * M // 2) for u in range(2)]
-        for u in range(2):
-            pick_difference(last, seconds[u], u * M // 2, (u + 1) * M // 2)
-            round_z(1, u * M // 2, (u + 1) * M // 2)
+        z_cuts = [(0, 256), (256, 384), (384, 512)]
+        seconds = [pick_second(last, m0, m1) for m0, m1 in z_cuts]
+        for second, (m0, m1) in zip(seconds, z_cuts):
+            pick_difference(last, second, m0, m1)
+            round_z(1, m0, m1, nc.scalar.copy)
         quantize(w3q[0, 1], w3_grouped[0, 1], 0, PASS)
-        quantize(zq[1], zg[1], 0, M // 2)
+        for m0, m1 in z_cuts:
+            quantize(zq[1], zg[1], m0, m1)
         quantize(w3q[1, 1], w3_grouped[1, 1], 0, PASS)
-        quantize(zq[1], zg[1], M // 2, M)
 
         out_tiles = out.rearrange("(b p t) j -> b t p j", b=2, t=PACK)
 
         def make_y(n):
             b, t = divmod(n, PACK)
             py = psum.tile([P, M], F32, name="py", tag="py", bufs=2)
-            for a in range(2):
+            passes = [(0, 0, M)] + ([(1, m0, m1) for m0, m1 in z_cuts] if n == 0 else [(1, 0, M)])
+            for a, m0, m1 in passes:
                 codes, scales = w3q[a, b]
                 nc.tensor.matmul_mx(
-                    out=py[:], lhsT=codes[:, t * P : (t + 1) * P].bitcast(E4M3),
+                    out=py[:, m0:m1], lhsT=codes[:, t * P : (t + 1) * P].bitcast(E4M3),
                     lhsT_scale=scales[:, t * P : (t + 1) * P],
-                    rhs=zq[a][0][:].bitcast(E4M3), rhs_scale=zq[a][1][:], start=(a == 0), stop=(a == 1),
+                    rhs=zq[a][0][:, m0:m1].bitcast(E4M3), rhs_scale=zq[a][1][:, m0:m1],
+                    start=(a == 0), stop=(a == 1 and m1 == M),
                 )
             y0 = (TILES - 1 - n) * M
             nc.scalar.copy(out=ys[:, y0 : y0 + M], in_=py[:])
 
-        pieces = [(n, 0, S) for n in range(TILES - 1)] + [(last, 0, S // 2), (last, S // 2, S)]
-        ups = {}
-        mags = {}
+        ups = [ring.tile([P, S], F32, name="up%d" % n, tag="up", bufs=6) for n in range(TILES)]
+        prods = {}
 
-        def pick_up(k):
-            n, j0, j1 = pieces[k]
+        def half(u):
+            return slice(u * BANK, (u + 1) * BANK)
+
+        def pick_up(n, j0, j1):
             y0 = (TILES - 1 - n) * M
-            up = ring.tile([P, S], F32, name="up", tag="up", bufs=4)
-            nc.vector.tensor_copy(up[:, 0 : j1 - j0], ys[:, y0 : y0 + Y_WINDOW].indirect(pos3_t[:, j0 // 16 : j1 // 16]))
-            mag = ring.tile([P, S], F32, name="mag", tag="mag", bufs=3)
-            nc.scalar.activation(mag[:, 0 : j1 - j0], up[:, 0 : j1 - j0], ACT.Abs)
-            ups[k], mags[k] = up, mag
+            nc.vector.tensor_copy(ups[n][:, j0:j1], ys[:, y0 : y0 + Y_WINDOW].indirect(pos3_t[:, j0 // 16 : j1 // 16]))
 
-        def scale_up(k):
-            n, j0, j1 = pieces[k]
-            b, t = divmod(n, PACK)
-            mag = mags[k][:, 0 : j1 - j0]
-            nc.vector.scalar_tensor_tensor(mag, mag, gain_t[:, b, t : t + 1], h[n][:, j0:j1], ALU.mult, ALU.mult)
+        def magnitude_in_psum(n, u):
+            turned = psum.tile([P, BANK], F32, name="turned", tag="pa", bufs=3)
+            for c in range(PACK):
+                j0 = u * BANK + c * P
+                nc.tensor.transpose(turned[:, c * P : (c + 1) * P], ups[n][:, j0 : j0 + P], ident[:])
+            mag_turned = ring.tile([P, BANK], F32, name="mag_turned", tag="mag", bufs=4)
+            nc.scalar.activation(mag_turned[:], turned[:], ACT.Abs)
+            mag = psum.tile([P, BANK], F32, name="mag", tag="pb", bufs=3)
+            for c in range(PACK):
+                nc.tensor.transpose(mag[:, c * P : (c + 1) * P], mag_turned[:, c * P : (c + 1) * P], ident[:])
+            return mag
 
-        def finish(k):
-            n, j0, j1 = pieces[k]
+        def magnitude_in_sbuf(n, u):
+            mag = ring.tile([P, BANK], F32, name="mag_plain", tag="mag", bufs=4)
+            nc.scalar.activation(mag[:], ups[n][:, half(u)], ACT.Abs)
+            return mag
+
+        def scale_up(n, u, mag):
             b, t = divmod(n, PACK)
-            up = ups[k][:, 0 : j1 - j0]
-            nc.vector.tensor_tensor(up, mags[k][:, 0 : j1 - j0], up, ALU.add)
-            nc.sync.dma_start(out=out_tiles[b, t][:, j0:j1], in_=up)
+            prod = ring.tile([P, BANK], F32, name="prod", tag="prod", bufs=6)
+            nc.vector.scalar_tensor_tensor(prod[:], mag[:], gain_t[:, b, t : t + 1], h[n][:, half(u)], ALU.mult, ALU.mult)
+            prods[n, u] = prod
+
+        def add_up(n, u, engine):
+            up = ups[n][:, half(u)]
+            engine.tensor_tensor(up, prods[n, u][:], up, ALU.add)
+
+        def store(n, j0, j1):
+            b, t = divmod(n, PACK)
+            nc.sync.dma_start(out=out_tiles[b, t][:, j0:j1], in_=ups[n][:, j0:j1])
 
         make_y(0)
         make_y(1)
-        for k in range(len(pieces) + 2):
-            if k + 2 < TILES:
-                make_y(k + 2)
-            if k < len(pieces):
-                pick_up(k)
-            if 2 <= k:
-                finish(k - 2)
-            if 1 <= k <= len(pieces):
-                scale_up(k - 1)
+        pick_up(0, 0, S)
+        mags = [magnitude_in_psum(0, u) for u in range(2)]
+        for n in range(TILES - 2):
+            make_y(n + 2)
+            pick_up(n + 1, 0, S)
+            for u in range(2):
+                scale_up(n, u, mags[u])
+                add_up(n, u, nc.gpsimd)
+                mags[u] = magnitude_in_psum(n + 1, u)
+            store(n, 0, S)
+        plain = []
+        for u in range(2):
+            pick_up(last, u * BANK, (u + 1) * BANK)
+            plain.append(magnitude_in_sbuf(last, u))
+            scale_up(last - 1, u, mags[u])
+        add_up(last - 1, 0, nc.gpsimd)
+        store(last - 1, 0, BANK)
+        scale_up(last, 0, plain[0])
+        add_up(last - 1, 1, nc.vector)
+        store(last - 1, BANK, S)
+        scale_up(last, 1, plain[1])
+        for u in range(2):
+            add_up(last, u, nc.vector)
+            store(last, u * BANK, (u + 1) * BANK)

@@ -126,8 +126,10 @@ def tile_list_loft_return_scores_kernel(
             nc.vector.tensor_copy(vw[u][:], tabw[:].bitcast(U32).indirect(offs_t[:, 32 * u : 32 * (u + 1)]))
 
         w2q = [mx_tiles("w2q%d" % b, PASS) for b in range(2)]
-        w3q = {(a, b): mx_tiles("w3q%d%d" % (a, b), PASS) for a in range(2) for b in range(2)}
         zq = [mx_tiles("zq%d" % a, M) for a in range(2)]
+        w3q = {part: mx_tiles("w3q%d%d" % part, PASS) for part in ((0, 0), (1, 0), (0, 1))}
+        w3q11_codes = keep.tile([P, PASS], U32, name="w3q11_codes", align_bytes=64)
+        w3q[1, 1] = w3q11_codes, zq[1][1][4:, :]
 
         grouped = round_weight(w2_raw[0], "w2_g0", [("v", 0, 80), ("s", 80, 128)])
         quantize(w2q[0], grouped, 0, P)
@@ -139,10 +141,19 @@ def tile_list_loft_return_scores_kernel(
         z32 = [keep.tile([P, PACK, M], F32, name="z32_%d" % a) for a in range(2)]
         zg = [keep.tile([P, PACK * M], BF16, name="zg%d" % a, align_bytes=64) for a in range(2)]
 
+        scalar_banks = [psum.tile([P, BANK], F32, name="scalar_bank%d" % e) for e in range(3)]
+        bank_uses = []
+        linear_banks = [psum.tile([P, BANK], F32, name="linear_bank%d" % e) for e in range(3)]
+
+        def scalar_bank():
+            bank = scalar_banks[len(bank_uses) % 3]
+            bank_uses.append(bank)
+            return bank
+
         def square_part(i, u):
             b, t = divmod(i, PACK)
             cols = slice(u * BANK, (u + 1) * BANK)
-            pb = psum.tile([P, BANK], F32, name="pb", tag="pb", bufs=3)
+            pb = scalar_bank()
             codes, scales = w2q[b]
             nc.tensor.matmul_mx(
                 out=pb[:], lhsT=codes[:, t * P : (t + 1) * P].bitcast(E4M3), lhsT_scale=scales[:, t * P : (t + 1) * P],
@@ -153,7 +164,7 @@ def tile_list_loft_return_scores_kernel(
         def linear_part(i, u):
             b, t = divmod(i, PACK)
             cols = slice(u * BANK, (u + 1) * BANK)
-            pa = psum.tile([P, BANK], F32, name="pa", tag="pa", bufs=3)
+            pa = linear_banks[(2 * i + u) % 3]
             nc.tensor.matmul_mx(
                 out=pa[:], lhsT=w4w[b][:, 2 * t * P : 2 * (t + 1) * P].bitcast(E2M1),
                 lhsT_scale=w4s[b][:, t * P : (t + 1) * P],
@@ -178,6 +189,20 @@ def tile_list_loft_return_scores_kernel(
                 out=zg[a][:, PACK * m0 : PACK * m1].rearrange("p (c i t) -> p c t i", i=4, t=PACK),
                 in_=z32[a][:, :, m0:m1].rearrange("p t (c i) -> p c t i", i=4),
             )
+
+        def half(u):
+            return slice(u * BANK, (u + 1) * BANK)
+
+        def turn(bank, tile, u):
+            for c in range(PACK):
+                j0 = u * BANK + c * P
+                nc.tensor.transpose(bank[:, c * P : (c + 1) * P], tile[:, j0 : j0 + P], ident[:])
+
+        y_banks = [psum.tile([P, BANK], F32, name="y_bank%d" % e) for e in range(2)]
+
+        def turn_h(i, u, bank):
+            turn(bank, h[i], u)
+            nc.scalar.copy(out=h[i][:, half(u)], in_=bank[:])
 
         whole = [("s", 0, P)]
         for u in range(2):
@@ -213,20 +238,21 @@ def tile_list_loft_return_scores_kernel(
                 quantize(zq[0], zg[0], 0, M)
         last = TILES - 1
         z_cuts = [(0, 256), (256, 384), (384, 512)]
-        seconds = [pick_second(last, m0, m1) for m0, m1 in z_cuts]
-        for second, (m0, m1) in zip(seconds, z_cuts):
-            pick_difference(last, second, m0, m1)
+        seconds = [pick_second(last, *z_cuts[0])]
+        for k, (m0, m1) in enumerate(z_cuts):
+            if k + 1 < len(z_cuts):
+                seconds.append(pick_second(last, *z_cuts[k + 1]))
+            pick_difference(last, seconds[k], m0, m1)
             round_z(1, m0, m1, nc.scalar.copy)
         quantize(w3q[0, 1], w3_grouped[0, 1], 0, PASS)
         for m0, m1 in z_cuts:
             quantize(zq[1], zg[1], m0, m1)
-        quantize(w3q[1, 1], w3_grouped[1, 1], 0, PASS)
 
         out_tiles = out.rearrange("(b p t) j -> b t p j", b=2, t=PACK)
 
         def make_y(n):
             b, t = divmod(n, PACK)
-            py = psum.tile([P, M], F32, name="py", tag="py", bufs=2)
+            py = y_banks[1 if n == 1 else 0]
             passes = [(0, 0, M)] + ([(1, m0, m1) for m0, m1 in z_cuts] if n == 0 else [(1, 0, M)])
             for a, m0, m1 in passes:
                 codes, scales = w3q[a, b]
@@ -239,70 +265,66 @@ def tile_list_loft_return_scores_kernel(
             y0 = (TILES - 1 - n) * M
             nc.scalar.copy(out=ys[:, y0 : y0 + M], in_=py[:])
 
-        ups = [ring.tile([P, S], F32, name="up%d" % n, tag="up", bufs=6) for n in range(TILES)]
-        prods = {}
+        lanes = [keep.tile([P, (3 if n < last - 2 else 2) * BANK], F32, name="lane%d" % n) for n in range(TILES)]
+        firsts = [keep.tile([P, S], F32, name="up%d" % n) for n in range(2)]
+        up_rows = [t[:] for t in firsts] + [lanes[n][:, BANK:] for n in range(last - 2)]
+        ups = {(n, u): up_rows[n][:, half(u)] for n in range(last) for u in range(2)}
+        for u in range(2):
+            ups[last, u] = lanes[last - 2 + u][:, BANK:]
+        mags = {(n, u): lanes[n][:, half(u)] for n in range(TILES) for u in range(2)}
 
-        def half(u):
-            return slice(u * BANK, (u + 1) * BANK)
-
-        def pick_up(n, j0, j1):
+        def pick_up(n):
             y0 = (TILES - 1 - n) * M
-            nc.vector.tensor_copy(ups[n][:, j0:j1], ys[:, y0 : y0 + Y_WINDOW].indirect(pos3_t[:, j0 // 16 : j1 // 16]))
+            nc.vector.tensor_copy(up_rows[n], ys[:, y0 : y0 + Y_WINDOW].indirect(pos3_t[:]))
+            nc.scalar.activation(lanes[n][:, 0:S], up_rows[n], ACT.Abs)
 
-        def magnitude_in_psum(n, u):
-            turned = psum.tile([P, BANK], F32, name="turned", tag="pa", bufs=3)
-            for c in range(PACK):
-                j0 = u * BANK + c * P
-                nc.tensor.transpose(turned[:, c * P : (c + 1) * P], ups[n][:, j0 : j0 + P], ident[:])
-            mag_turned = ring.tile([P, BANK], F32, name="mag_turned", tag="mag", bufs=4)
-            nc.scalar.activation(mag_turned[:], turned[:], ACT.Abs)
-            mag = psum.tile([P, BANK], F32, name="mag", tag="pb", bufs=3)
-            for c in range(PACK):
-                nc.tensor.transpose(mag[:, c * P : (c + 1) * P], mag_turned[:, c * P : (c + 1) * P], ident[:])
-            return mag
+        def pick_up_last(u):
+            nc.vector.tensor_copy(ups[last, u], ys[:, 0:Y_WINDOW].indirect(pos3_t[:, 32 * u : 32 * (u + 1)]))
+            nc.scalar.activation(mags[last, u], ups[last, u], ACT.Abs)
 
-        def magnitude_in_sbuf(n, u):
-            mag = ring.tile([P, BANK], F32, name="mag_plain", tag="mag", bufs=4)
-            nc.scalar.activation(mag[:], ups[n][:, half(u)], ACT.Abs)
-            return mag
-
-        def scale_up(n, u, mag):
+        def scale_up(n, u):
             b, t = divmod(n, PACK)
-            prod = ring.tile([P, BANK], F32, name="prod", tag="prod", bufs=6)
-            nc.vector.scalar_tensor_tensor(prod[:], mag[:], gain_t[:, b, t : t + 1], h[n][:, half(u)], ALU.mult, ALU.mult)
-            prods[n, u] = prod
+            if (n, u) in turned:
+                h_bank = scalar_bank()
+                turn(h_bank, h[n], u)
+                source = h_bank[:]
+            else:
+                source = h[n][:, half(u)]
+            nc.vector.scalar_tensor_tensor(
+                h[n][:, half(u)], source, gain_t[:, b, t : t + 1], mags[n, u], ALU.mult, ALU.mult
+            )
 
         def add_up(n, u, engine):
-            up = ups[n][:, half(u)]
-            engine.tensor_tensor(up, prods[n, u][:], up, ALU.add)
+            engine.tensor_tensor(h[n][:, half(u)], h[n][:, half(u)], ups[n, u], ALU.add)
 
-        def store(n, j0, j1):
+        def store(n, j0, j1, queue):
             b, t = divmod(n, PACK)
-            nc.sync.dma_start(out=out_tiles[b, t][:, j0:j1], in_=ups[n][:, j0:j1])
+            queue.dma_start(out=out_tiles[b, t][:, j0:j1], in_=h[n][:, j0:j1])
 
+        turned = [(n, 1) for n in range(1, last)] + [(last - 1, 0), (last, 0)]
         make_y(0)
+        quantize(w3q[1, 1], w3_grouped[1, 1], 0, PASS)
         make_y(1)
-        pick_up(0, 0, S)
-        mags = [magnitude_in_psum(0, u) for u in range(2)]
+        pick_up(0)
         for n in range(TILES - 2):
             make_y(n + 2)
-            pick_up(n + 1, 0, S)
-            for u in range(2):
-                scale_up(n, u, mags[u])
+            pick_up(n + 1)
+            for k in range(2 * n, min(2 * n + 2, 8)):
+                turn_h(*turned[k], y_banks[1] if k and k % 2 == 0 else linear_banks[0])
+            for u in (1, 0):
+                scale_up(n, u)
                 add_up(n, u, nc.gpsimd)
-                mags[u] = magnitude_in_psum(n + 1, u)
-            store(n, 0, S)
-        plain = []
-        for u in range(2):
-            pick_up(last, u * BANK, (u + 1) * BANK)
-            plain.append(magnitude_in_sbuf(last, u))
-            scale_up(last - 1, u, mags[u])
-        add_up(last - 1, 0, nc.gpsimd)
-        store(last - 1, 0, BANK)
-        scale_up(last, 0, plain[0])
-        add_up(last - 1, 1, nc.vector)
-        store(last - 1, BANK, S)
-        scale_up(last, 1, plain[1])
+            store(n, 0, S, nc.sync)
+        pick_up_last(0)
+        for u in (1, 0):
+            scale_up(last - 1, u)
+        add_up(last - 1, 1, nc.gpsimd)
+        store(last - 1, BANK, S, nc.sync)
+        pick_up_last(1)
+        scale_up(last, 0)
+        add_up(last - 1, 0, nc.vector)
+        store(last - 1, 0, BANK, nc.scalar)
+        scale_up(last, 1)
         for u in range(2):
             add_up(last, u, nc.vector)
-            store(last, u * BANK, (u + 1) * BANK)
+            store(last, u * BANK, (u + 1) * BANK, nc.scalar)

from contextlib import ExitStack

import concourse.mybir as mybir
from concourse.masks import make_identity

K, H, T, S, M = 512, 1024, 4096, 1024, 512
FLOPS = 2 * (2 * K * H * S + H * H * M)

F32 = mybir.dt.float32
BF16 = mybir.dt.bfloat16
I32 = mybir.dt.int32
U32 = mybir.dt.uint32
U16 = mybir.dt.uint16
U8 = mybir.dt.uint8
E4M3 = mybir.dt.float8_e4m3fn_x4
E2M1 = mybir.dt.float4_e2m1fn_x4
ALU = mybir.AluOpType
ACT = mybir.ActivationFunctionType

P = 128
PACK = 4
PASS = P * PACK
BANK = 512
TILES = H // P
Y_WINDOW = 1536


def tile_list_loft_return_scores_kernel(
    tc, tab_words, tab_scales, offs, w4_words, w4_scales, w2, pos1, pos2, w3, pos3, gain, out
):
    nc = tc.nc
    with ExitStack() as ctx:
        keep = ctx.enter_context(tc.tile_pool(name="keep", bufs=1))
        ring = ctx.enter_context(tc.tile_pool(name="ring", bufs=2))
        psum = ctx.enter_context(tc.psum_pool(name="psum", bufs=1))

        offs_t = keep.tile([P, S // 16], U16, name="offs_t")
        pos1_t = keep.tile([P, M // 16], U16, name="pos1_t")
        pos2_t = keep.tile([P, M // 16], U16, name="pos2_t")
        pos3_t = keep.tile([P, S // 16], U16, name="pos3_t")
        tabw = keep.tile([P, T], I32, name="tabw", align_bytes=64)
        tabs = keep.tile([P, T], U8, name="tabs", align_bytes=64)
        w4w_raw = keep.tile([P, 2 * H], U8, name="w4w_raw", align_bytes=64)
        w4s_raw = keep.tile([P, H], U8, name="w4s_raw", align_bytes=64)
        gain_t = keep.tile([P, 2, PACK], F32, name="gain_t")
        ys = keep.tile([P, (TILES - 1) * M + Y_WINDOW], F32, name="ys")

        nc.gpsimd.memset(tabs[:].bitcast(I32)[:, 0:640], 0)
        nc.vector.memset(tabs[:].bitcast(I32)[:, 640:], 0)
        nc.gpsimd.memset(w4s_raw[:].bitcast(I32), 0)
        nc.sync.dma_start(offs_t[:], offs)
        nc.sync.dma_start(out=w4w_raw[:].bitcast(I32), in_=w4_words[0].bitcast(I32))

        def load_scale_rows(engine, plane, rows):
            for q in range(4):
                engine.dma_start(
                    out=plane[32 * q : 32 * q + 4, :].bitcast(I32), in_=rows[0, 4 * q : 4 * q + 4, :].bitcast(I32)
                )

        load_scale_rows(nc.sync, tabs, tab_scales)
        nc.sync.dma_start(out=tabw[:], in_=tab_words[0].rearrange("p t i -> p (t i)").bitcast(I32))
        nc.gpsimd.memset(ys[:, TILES * M :], 0.0)
        ident = keep.tile([P, P], F32, name="ident")
        make_identity(nc, ident[:])

        def load_weight(rows, b, name):
            raw = ring.tile([P, PACK, PASS], F32, name=name, tag="raw", bufs=4)
            nc.sync.dma_start(
                out=raw[:], in_=rows.rearrange("(p j) n -> p j n", j=PACK)[:, :, b * PASS : (b + 1) * PASS]
            )
            return raw

        def round_weight(raw, name, split):
            grouped = ring.tile([P, PACK * PASS], BF16, name=name, tag="grouped", bufs=4, align_bytes=64)
            dst = grouped[:].rearrange("p (t q j) -> p q j t", t=PACK, j=PACK)
            src = raw[:].rearrange("p j (q t) -> p q j t", t=PACK)
            for engine, q0, q1 in split:
                if engine == "v":
                    nc.vector.tensor_copy(out=dst[:, q0:q1], in_=src[:, q0:q1])
                else:
                    nc.scalar.copy(out=dst[:, q0:q1], in_=src[:, q0:q1])
            return grouped

        def mx_tiles(name, cols):
            codes = keep.tile([P, cols], U32, name=name + "_codes", align_bytes=64)
            scales = keep.tile([P, cols], U8, name=name + "_scales", align_bytes=64)
            return codes, scales

        def quantize(mx, grouped, c0, c1):
            codes, scales = mx
            nc.vector.quantize_mx(
                out=codes[:, c0:c1].bitcast(E4M3), scales=scales[:, c0:c1], in_=grouped[:, PACK * c0 : PACK * c1]
            )

        w2_raw = [load_weight(w2, 0, "w2_raw0")]
        load_scale_rows(nc.sync, w4s_raw, w4_scales)
        w2_raw.append(load_weight(w2, 1, "w2_raw1"))
        nc.sync.dma_start(pos2_t[:], pos2)
        nc.sync.dma_start(pos1_t[:], pos1)
        w3_raw = {}
        for b in range(2):
            for a in range(2):
                w3_raw[a, b] = load_weight(w3[a * PASS : (a + 1) * PASS, :], b, "w3_raw%d%d" % (a, b))
            if b == 0:
                nc.sync.dma_start(pos3_t[:], pos3)
                nc.sync.dma_start(out=gain_t[:], in_=gain.rearrange("(b p t) -> p b t", b=2, t=PACK))

        w4w = [keep.tile([P, 2 * PASS], U8, name="w4w%d" % b, align_bytes=64) for b in range(2)]
        w4s = [keep.tile([P, PASS], U8, name="w4s%d" % b, align_bytes=64) for b in range(2)]
        for b in range(2):
            nc.vector.tensor_copy(
                out=w4w[b][:].bitcast(U16).rearrange("p (t q) -> p t q", t=PACK),
                in_=w4w_raw[:, 2 * PASS * b : 2 * PASS * (b + 1)].bitcast(U16).rearrange("p (q t) -> p t q", t=PACK),
            )

        def deal_w4_scales(b):
            nc.vector.tensor_copy(
                out=w4s[b][:].rearrange("p (t q) -> p t q", t=PACK),
                in_=w4s_raw[:, PASS * b : PASS * (b + 1)].rearrange("p (q t) -> p t q", t=PACK),
            )

        vw = [keep.tile([P, BANK], U32, name="vw%d" % u, align_bytes=64) for u in range(2)]
        vs = keep.tile([P, S], U8, name="vs", align_bytes=64)
        nc.vector.tensor_copy(vs[:], tabs[:].indirect(offs_t[:]))
        for u in range(2):
            nc.vector.tensor_copy(vw[u][:], tabw[:].bitcast(U32).indirect(offs_t[:, 32 * u : 32 * (u + 1)]))

        w2q = [mx_tiles("w2q%d" % b, PASS) for b in range(2)]
        zq = [mx_tiles("zq%d" % a, M) for a in range(2)]
        w3q = {part: mx_tiles("w3q%d%d" % part, PASS) for part in ((0, 0), (1, 0), (0, 1))}
        w3q11_codes = keep.tile([P, PASS], U32, name="w3q11_codes", align_bytes=64)
        w3q[1, 1] = w3q11_codes, zq[1][1][4:, :]

        grouped = round_weight(w2_raw[0], "w2_g0", [("v", 0, 80), ("s", 80, 128)])
        quantize(w2q[0], grouped, 0, P)
        deal_w4_scales(0)
        quantize(w2q[0], grouped, P, 2 * P)
        quantize(w2q[0], grouped, 2 * P, 4 * P)

        h = [keep.tile([P, S], F32, name="h%d" % i) for i in range(TILES)]
        z32 = [keep.tile([P, PACK, M], F32, name="z32_%d" % a) for a in range(2)]
        zg = [keep.tile([P, PACK * M], BF16, name="zg%d" % a, align_bytes=64) for a in range(2)]

        scalar_banks = [psum.tile([P, BANK], F32, name="scalar_bank%d" % e) for e in range(3)]
        bank_uses = []
        linear_banks = [psum.tile([P, BANK], F32, name="linear_bank%d" % e) for e in range(3)]

        def scalar_bank():
            bank = scalar_banks[len(bank_uses) % 3]
            bank_uses.append(bank)
            return bank

        def square_part(i, u):
            b, t = divmod(i, PACK)
            cols = slice(u * BANK, (u + 1) * BANK)
            pb = scalar_bank()
            codes, scales = w2q[b]
            nc.tensor.matmul_mx(
                out=pb[:], lhsT=codes[:, t * P : (t + 1) * P].bitcast(E4M3), lhsT_scale=scales[:, t * P : (t + 1) * P],
                rhs=vw[u][:].bitcast(E4M3), rhs_scale=vs[:, cols], start=True, stop=True,
            )
            nc.scalar.activation(h[i][:, cols], pb[:], ACT.Square)

        def linear_part(i, u):
            b, t = divmod(i, PACK)
            cols = slice(u * BANK, (u + 1) * BANK)
            pa = linear_banks[(2 * i + u) % 3]
            nc.tensor.matmul_mx(
                out=pa[:], lhsT=w4w[b][:, 2 * t * P : 2 * (t + 1) * P].bitcast(E2M1),
                lhsT_scale=w4s[b][:, t * P : (t + 1) * P],
                rhs=vw[u][:].bitcast(E4M3), rhs_scale=vs[:, cols], start=True, stop=True,
            )
            nc.vector.tensor_tensor(h[i][:, cols], pa[:], h[i][:, cols], ALU.add)

        def pick_second(i, m0, m1):
            second = ring.tile([P, M], F32, name="second", tag="second", bufs=3)
            nc.vector.tensor_copy(second[:, 0 : m1 - m0], h[i][:].indirect(pos2_t[:, m0 // 16 : m1 // 16]))
            return second

        def pick_difference(i, second, m0, m1):
            b, t = divmod(i, PACK)
            nc.vector.tensor_tensor(
                z32[b][:, t, m0:m1], h[i][:].indirect(pos1_t[:, m0 // 16 : m1 // 16]), second[:, 0 : m1 - m0],
                ALU.subtract,
            )

        def round_z(a, m0, m1, copy):
            copy(
                out=zg[a][:, PACK * m0 : PACK * m1].rearrange("p (c i t) -> p c t i", i=4, t=PACK),
                in_=z32[a][:, :, m0:m1].rearrange("p t (c i) -> p c t i", i=4),
            )

        def half(u):
            return slice(u * BANK, (u + 1) * BANK)

        def turn(bank, tile, u):
            for c in range(PACK):
                j0 = u * BANK + c * P
                nc.tensor.transpose(bank[:, c * P : (c + 1) * P], tile[:, j0 : j0 + P], ident[:])

        y_banks = [psum.tile([P, BANK], F32, name="y_bank%d" % e) for e in range(2)]

        def turn_h(i, u, bank):
            turn(bank, h[i], u)
            nc.scalar.copy(out=h[i][:, half(u)], in_=bank[:])

        whole = [("s", 0, P)]
        for u in range(2):
            square_part(0, u)
            linear_part(0, u)
        for u in range(2):
            square_part(1, u)
        w2_grouped = round_weight(w2_raw[1], "w2_g1", whole)
        for i in (2, 3):
            for u in range(2):
                square_part(i, u)
        w3_grouped = {}
        for i in range(TILES - 1):
            linear_part(i + 1, 0)
            second = pick_second(i, 0, M)
            linear_part(i + 1, 1)
            pick_difference(i, second, 0, M)
            if i == 0:
                quantize(w2q[1], w2_grouped, 0, PASS)
                deal_w4_scales(1)
                for r in range(PACK, TILES):
                    for u in range(2):
                        square_part(r, u)
                for a in range(2):
                    w3_grouped[a, 0] = round_weight(w3_raw[a, 0], "w3_g%d0" % a, whole)
            if i == 3:
                round_z(0, 0, M, nc.scalar.copy)
                for a in range(2):
                    w3_grouped[a, 1] = round_weight(w3_raw[a, 1], "w3_g%d1" % a, whole)
            if i in (3, 4):
                quantize(w3q[i - 3, 0], w3_grouped[i - 3, 0], 0, PASS)
            if i == 5:
                quantize(zq[0], zg[0], 0, M)
        last = TILES - 1
        z_cuts = [(0, 256), (256, 384), (384, 512)]
        seconds = [pick_second(last, *z_cuts[0])]
        for k, (m0, m1) in enumerate(z_cuts):
            if k + 1 < len(z_cuts):
                seconds.append(pick_second(last, *z_cuts[k + 1]))
            pick_difference(last, seconds[k], m0, m1)
            round_z(1, m0, m1, nc.scalar.copy)
        quantize(w3q[0, 1], w3_grouped[0, 1], 0, PASS)
        for m0, m1 in z_cuts:
            quantize(zq[1], zg[1], m0, m1)

        out_tiles = out.rearrange("(b p t) j -> b t p j", b=2, t=PACK)

        def make_y(n):
            b, t = divmod(n, PACK)
            py = y_banks[1 if n == 1 else 0]
            passes = [(0, 0, M)] + ([(1, m0, m1) for m0, m1 in z_cuts] if n == 0 else [(1, 0, M)])
            for a, m0, m1 in passes:
                codes, scales = w3q[a, b]
                nc.tensor.matmul_mx(
                    out=py[:, m0:m1], lhsT=codes[:, t * P : (t + 1) * P].bitcast(E4M3),
                    lhsT_scale=scales[:, t * P : (t + 1) * P],
                    rhs=zq[a][0][:, m0:m1].bitcast(E4M3), rhs_scale=zq[a][1][:, m0:m1],
                    start=(a == 0), stop=(a == 1 and m1 == M),
                )
            y0 = (TILES - 1 - n) * M
            nc.scalar.copy(out=ys[:, y0 : y0 + M], in_=py[:])

        lanes = [keep.tile([P, (3 if n < last - 2 else 2) * BANK], F32, name="lane%d" % n) for n in range(TILES)]
        firsts = [keep.tile([P, S], F32, name="up%d" % n) for n in range(2)]
        up_rows = [t[:] for t in firsts] + [lanes[n][:, BANK:] for n in range(last - 2)]
        ups = {(n, u): up_rows[n][:, half(u)] for n in range(last) for u in range(2)}
        for u in range(2):
            ups[last, u] = lanes[last - 2 + u][:, BANK:]
        mags = {(n, u): lanes[n][:, half(u)] for n in range(TILES) for u in range(2)}

        def pick_up(n):
            y0 = (TILES - 1 - n) * M
            nc.vector.tensor_copy(up_rows[n], ys[:, y0 : y0 + Y_WINDOW].indirect(pos3_t[:]))
            nc.scalar.activation(lanes[n][:, 0:S], up_rows[n], ACT.Abs)

        def pick_up_last(u):
            nc.vector.tensor_copy(ups[last, u], ys[:, 0:Y_WINDOW].indirect(pos3_t[:, 32 * u : 32 * (u + 1)]))
            nc.scalar.activation(mags[last, u], ups[last, u], ACT.Abs)

        def scale_up(n, u):
            b, t = divmod(n, PACK)
            if (n, u) in turned:
                h_bank = scalar_bank()
                turn(h_bank, h[n], u)
                source = h_bank[:]
            else:
                source = h[n][:, half(u)]
            nc.vector.scalar_tensor_tensor(
                h[n][:, half(u)], source, gain_t[:, b, t : t + 1], mags[n, u], ALU.mult, ALU.mult
            )

        def add_up(n, u, engine):
            engine.tensor_tensor(h[n][:, half(u)], h[n][:, half(u)], ups[n, u], ALU.add)

        def store(n, j0, j1, queue):
            b, t = divmod(n, PACK)
            queue.dma_start(out=out_tiles[b, t][:, j0:j1], in_=h[n][:, j0:j1])

        turned = [(n, 1) for n in range(1, last)] + [(last - 1, 0), (last, 0)]
        make_y(0)
        quantize(w3q[1, 1], w3_grouped[1, 1], 0, PASS)
        make_y(1)
        pick_up(0)
        for n in range(TILES - 2):
            make_y(n + 2)
            pick_up(n + 1)
            for k in range(2 * n, min(2 * n + 2, 8)):
                turn_h(*turned[k], y_banks[1] if k and k % 2 == 0 else linear_banks[0])
            for u in (1, 0):
                scale_up(n, u)
                add_up(n, u, nc.gpsimd)
            store(n, 0, S, nc.sync)
        pick_up_last(0)
        for u in (1, 0):
            scale_up(last - 1, u)
        add_up(last - 1, 1, nc.gpsimd)
        store(last - 1, BANK, S, nc.sync)
        pick_up_last(1)
        scale_up(last, 0)
        add_up(last - 1, 0, nc.vector)
        store(last - 1, 0, BANK, nc.scalar)
        scale_up(last, 1)
        for u in range(2):
            add_up(last, u, nc.vector)
            store(last, u * BANK, (u + 1) * BANK, nc.scalar)
